import numpy as np
import ml_dtypes


def mxq(x, axis, fmt="e4m3"):
    dtype, down = {"e4m3": (ml_dtypes.float8_e4m3fn, 7), "e5m2": (ml_dtypes.float8_e5m2, 14)}[fmt]
    v = np.moveaxis(np.asarray(x, np.float32).astype(ml_dtypes.bfloat16).astype(np.float64), axis, -1)
    blocks = v.reshape(v.shape[:-1] + (-1, 32))
    amax = np.abs(blocks).max(-1, keepdims=True)
    byte = np.maximum(np.where(amax > 0, np.frexp(amax)[1] - 1 + 127, 0) - down, 1)
    scale = np.exp2(byte - 127.0)
    codes = (blocks / scale).astype(np.float32).astype(dtype).astype(np.float64)
    return np.moveaxis((codes * scale).reshape(v.shape), -1, axis)


WIDE = False


def mx_kscale(k):
    if not WIDE:
        return np.ones(k)
    levels = np.array([10, -10, 5, -5, 0])
    if k % 512:
        return np.exp2(np.random.permutation(np.resize(levels, k // 32))).repeat(32)
    a = np.empty((k // 512, 16))
    for p in range(k // 512):
        a[p, :8] = np.random.permutation(np.resize(levels, 8))
        for g in range(8):
            far = levels[np.abs(levels - a[p, g]) >= 10]
            a[p, g + 8] = far[np.random.randint(len(far))]
    return np.exp2(a.ravel()).repeat(32)


BF16 = ml_dtypes.bfloat16


def bf(x):
    return np.asarray(x, np.float32).astype(BF16)


def f64(x):
    return np.asarray(x).astype(np.float64)

def planes(Y):
    n, m = Y.shape
    b = f64(bf(Y)).reshape(n // 32, 32, m)
    amax = np.abs(b).max(1)
    byte = np.clip(np.where(amax > 0, np.frexp(amax)[1] - 1 + 127 - 7, 1), 1, 254)
    codes = (b * np.exp2(127.0 - byte)[:, None, :]).reshape(n, m).astype(np.float32).astype(ml_dtypes.float8_e4m3fn).view(np.uint8)
    words = codes.reshape(n // 512, 128, 4, m).transpose(0, 1, 3, 2)
    return np.ascontiguousarray(words), np.ascontiguousarray(byte.astype(np.uint8).reshape(n // 512, 16, m))


R, G, T, D, F = 2, 2, 1024, 512, 512

THRESHOLD = 0.1


def setup_inputs():
    s, t = mx_kscale(D), mx_kscale(F)
    return {"x": bf(np.random.standard_normal((R, G, T, D)) * s),
            "w1": bf(0.7 * np.random.standard_normal((R, G, D, F)) / np.sqrt(D) / s[:, None] * t),
            "b1": bf(0.3 * np.random.standard_normal((R, G, F)) * t),
            "w2": bf(np.random.standard_normal((R, G, F, D)) / np.sqrt(F) / t[:, None]),
            "b2": bf(0.3 * np.random.standard_normal((R, G, D)))}


def complex_block_affine(re, im, w, b):
    rq = mxq(re, 2, "e4m3")
    iq = mxq(im, 2, "e4m3")
    wq = mxq(w, 2, "e4m3")
    out_re = (rq @ wq[0]) - (iq @ wq[1]) + b[0][:, None, :]
    out_im = (rq @ wq[1]) + (iq @ wq[0]) + b[1][:, None, :]
    return out_re, out_im


def soft_shrink(z):
    return np.maximum(z - THRESHOLD, 0.0) + np.minimum(z + THRESHOLD, 0.0)


def core(x, w1, b1, w2, b2):
    x, w1, b1, w2, b2 = f64(x), f64(w1), f64(b1), f64(w2), f64(b2)
    pre_re, pre_im = complex_block_affine(x[0], x[1], w1, b1)
    hr = np.maximum(pre_re, 0.0)
    hi = np.maximum(pre_im, 0.0)
    yr, yi = complex_block_affine(hr, hi, w2, b2)
    z = np.stack([yr, yi], axis=0)
    return soft_shrink(z)


def reference(x, w1, b1, w2, b2):
    R_out = core(x, w1, b1, w2, b2)
    words, scales = planes(np.moveaxis(R_out, 2, 0).reshape(1024, -1))
    return R_out, words, scales

@@ -1,0 +1,230 @@
+from contextlib import ExitStack
+
+import concourse.mybir as mybir
+from concourse.masks import make_identity
+
+R, G, T, D, F = 2, 2, 1024, 512, 512
+FLOPS = 2 * 8 * G * T * D * F
+F32 = mybir.dt.float32
+BF16 = mybir.dt.bfloat16
+U32 = mybir.dt.uint32
+I32 = mybir.dt.int32
+U8 = mybir.dt.uint8
+FP8X4 = mybir.dt.float8_e4m3fn_x4
+ALU = mybir.AluOpType
+ACT = mybir.ActivationFunctionType
+P = 128
+THR = 0.1
+
+
+def tile_afnocomplexblockspectralmlp_x1_kernel(tc, x, w1, b1, w2, b2, out_0, out_1, out_2):
+    nc = tc.nc
+    with ExitStack() as ctx:
+        const = ctx.enter_context(tc.tile_pool(name="const", bufs=1))
+        xin = ctx.enter_context(tc.tile_pool(name="xin", bufs=8))
+        win = ctx.enter_context(tc.tile_pool(name="win", bufs=6))
+        wst = ctx.enter_context(tc.tile_pool(name="wst", bufs=2))
+        st = ctx.enter_context(tc.tile_pool(name="st", bufs=2))
+        st3 = ctx.enter_context(tc.tile_pool(name="st3", bufs=3))
+        st4 = ctx.enter_context(tc.tile_pool(name="st4", bufs=4))
+        ps_x = ctx.enter_context(tc.psum_pool(name="ps_x", bufs=2))
+        ps_1 = ctx.enter_context(tc.psum_pool(name="ps_1", bufs=3))
+        ps_2 = ctx.enter_context(tc.psum_pool(name="ps_2", bufs=3))
+
+        ident = const.tile([P, P], F32, name="ident")
+        make_identity(nc, ident[:])
+
+        wraw = {}
+        xraw = {}
+
+        def load_w(layer, r, g):
+            w = w1 if layer == 1 else w2
+            t_ = win.tile([P, 4, 512], BF16, name="wraw")
+            nc.sync.dma_start(out=t_[:], in_=w[r, g, :, :].rearrange("(p j) c -> p j c", j=4))
+            wraw[layer, r, g] = t_
+
+        def load_x(r, g, a):
+            t_ = xin.tile([P, 4, 512], BF16, name="xraw")
+            nc.sync.dma_start(out=t_[:], in_=x[r, g, 512 * a : 512 * a + 512, :].rearrange("(p t) k -> p t k", t=4))
+            xraw[r, g, a] = t_
+
+        load_w(1, 0, 0)
+        load_x(0, 0, 0)
+        load_w(1, 1, 0)
+        load_x(1, 0, 0)
+        b1b = const.tile([P, 4, 4], BF16, name="b1b")
+        nc.sync.dma_start(out=b1b[:], in_=b1.rearrange("r g (p t) -> p (r g) t", t=4))
+        load_w(2, 0, 0)
+        load_w(2, 1, 0)
+        b2b = const.tile([P, 2048], BF16, name="b2b")
+        nc.sync.dma_start(out=b2b[:], in_=b2.rearrange("r g d -> (r g d)").partition_broadcast(P))
+        load_x(0, 0, 1)
+        load_x(1, 0, 1)
+        load_w(1, 0, 1)
+        load_w(1, 1, 1)
+        load_x(0, 1, 0)
+        load_x(1, 1, 0)
+        load_w(2, 0, 1)
+        load_w(2, 1, 1)
+        load_x(0, 1, 1)
+        load_x(1, 1, 1)
+
+        b1f = const.tile([P, 16], F32, name="b1f")
+        nc.vector.tensor_copy(out=b1f[:], in_=b1b[:].rearrange("p a t -> p (a t)"))
+
+        wq = {}
+
+        def quant(codes, scales, grouped):
+            nc.vector.quantize_mx(
+                out=codes[:].bitcast(FP8X4), scales=scales[:], in_=grouped[:].rearrange("p n j -> p (n j)")
+            )
+
+        def interleave4(eng, out, in_):
+            interleave(eng, out.rearrange("p (c i) t -> p c t i", i=4), in_.rearrange("p t (c i) -> p c t i", i=4))
+
+        def interleave(eng, out, in_):
+            if eng == "v":
+                nc.vector.tensor_copy(out=out, in_=in_)
+            else:
+                nc.scalar.copy(out=out, in_=in_)
+
+        def prep_w(layer, g, engs):
+            for r in range(2):
+                eng = engs[r]
+                raw = wraw[layer, r, g]
+                wg = wst.tile([P, 512, 4], BF16, name="wg", align_bytes=64)
+                if layer == 1:
+                    dst = wg[:].rearrange("p (t m) j -> p t m j", t=4)
+                    src = raw[:].rearrange("p j (m t) -> p t m j", t=4)
+                    interleave(eng, dst, src)
+                else:
+                    interleave4(eng, wg[:], raw[:])
+                c_ = const.tile([P, 512], U32, name="wc%d%d%d" % (layer, r, g), align_bytes=64)
+                s_ = const.tile([P, 512], U8, name="ws%d%d%d" % (layer, r, g), align_bytes=64)
+                quant(c_, s_, wg)
+                wq[layer, r, g] = (c_, s_)
+                if r == 1:
+                    wn = wst.tile([P, 512, 4], BF16, name="wn", align_bytes=64)
+                    nc.vector.tensor_scalar_mul(out=wn[:], in0=wg[:], scalar1=-1.0)
+                    c_ = const.tile([P, 512], U32, name="wcn%d%d" % (layer, g), align_bytes=64)
+                    s_ = const.tile([P, 512], U8, name="wsn%d%d" % (layer, g), align_bytes=64)
+                    quant(c_, s_, wn)
+                    wq[layer, 2, g] = (c_, s_)
+
+        xq = {}
+
+        def stage_x(g, a):
+            for r in range(2):
+                words = xraw[r, g, a][:].bitcast(F32)
+                xg = st.tile([P, 512, 4], BF16, name="xg", align_bytes=64)
+                xgw = xg[:].bitcast(F32)
+                for h in range(2):
+                    xt = ps_x.tile([P, 2, 2, P], F32, name="xt")
+                    for b in range(2):
+                        for u in range(2):
+                            nc.tensor.transpose(xt[:, b, u, :], words[:, 2 * h + b, u:256:2], ident[:])
+                    nc.scalar.copy(
+                        out=xgw[:, 256 * h : 256 * h + 256, :].rearrange("p (b n) u -> p b n u", b=2),
+                        in_=xt[:].rearrange("p b u n -> p b n u"),
+                    )
+                c_ = st4.tile([P, 512], U32, name="xc", align_bytes=64)
+                s_ = st4.tile([P, 512], U8, name="xs", align_bytes=64)
+                quant(c_, s_, xg)
+                xq[r, g, a] = (c_, s_)
+
+        def mm(out, lhs, lcols, rhs, first, last):
+            nc.tensor.matmul_mx(
+                out=out,
+                lhsT=lhs[0][:, lcols].bitcast(FP8X4),
+                lhsT_scale=lhs[1][:, lcols],
+                rhs=rhs[0][:].bitcast(FP8X4),
+                rhs_scale=rhs[1][:],
+                start=first,
+                stop=last,
+            )
+
+        hq = {}
+
+        def stage_1(g, a, on_v=(), hint="vs"):
+            for r in range(2):
+                hraw = st3.tile([P, 4, 512], BF16, name="hraw")
+                wa, wb = ((1, 0, g), (1, 2, g)) if r == 0 else ((1, 1, g), (1, 0, g))
+                for t in range(4):
+                    cols = slice(P * t, P * t + P)
+                    acc = ps_1.tile([P, 512], F32, name="acc1")
+                    mm(acc[:], wq[wa], cols, xq[0, g, a], True, False)
+                    mm(acc[:], wq[wb], cols, xq[1, g, a], False, True)
+                    i = (r * G + g) * 4 + t
+                    if (r, t) in on_v:
+                        nc.vector.tensor_scalar(
+                            out=hraw[:, t, :], in0=acc[:], scalar1=b1f[:, i : i + 1], scalar2=0.0, op0=ALU.add, op1=ALU.max
+                        )
+                    else:
+                        nc.scalar.activation(out=hraw[:, t, :], in_=acc[:], func=ACT.Relu, bias=b1f[:, i : i + 1])
+                hg = st.tile([P, 512, 4], BF16, name="hg", align_bytes=64)
+                interleave4(hint[r], hg[:], hraw[:])
+                c_ = st4.tile([P, 512], U32, name="hc", align_bytes=64)
+                s_ = st4.tile([P, 512], U8, name="hs", align_bytes=64)
+                quant(c_, s_, hg)
+                hq[r, g, a] = (c_, s_)
+
+        def stage_2(g, a, p_eng=("vv", "ss"), yi=("ss", "ss")):
+            ysc = st4.tile([P, 2, 512], U8, name="ysc", align_bytes=64)
+            for r in range(2):
+                wa, wb = ((2, 0, g), (2, 2, g)) if r == 0 else ((2, 1, g), (2, 0, g))
+                z = st3.tile([P, 4, 512], F32, name="z")
+                y = st4.tile([P, 4, 512], F32, name="y")
+                m0 = (r * G + g) * 512
+                for t in range(4):
+                    cols = slice(P * t, P * t + P)
+                    acc = ps_2.tile([P, 512], F32, name="acc2")
+                    mm(acc[:], hq[0, g, a], cols, wq[wa], True, False)
+                    mm(acc[:], hq[1, g, a], cols, wq[wb], False, True)
+                    nc.vector.tensor_tensor(out=z[:, t, :], in0=acc[:], in1=b2b[:, m0 : m0 + 512], op=ALU.add)
+                    if t % 2 == 1:
+                        h = slice(t - 1, t + 1)
+                        if p_eng[r][t // 2] == "v":
+                            nc.vector.tensor_scalar(
+                                out=y[:, h, :], in0=z[:, h, :], scalar1=-THR, scalar2=0.0, op0=ALU.add, op1=ALU.max
+                            )
+                        else:
+                            nc.scalar.activation(out=y[:, h, :], in_=z[:, h, :], func=ACT.Relu, bias=-THR)
+                        nc.vector.scalar_tensor_tensor(
+                            out=y[:, h, :], in0=z[:, h, :], scalar=THR, in1=y[:, h, :], op0=ALU.add, op1=ALU.min
+                        )
+                nc.sync.dma_start(
+                    out=out_0[r, g, 512 * a : 512 * a + 512, :].rearrange("(p t) d -> p t d", t=4), in_=y[:]
+                )
+                yg = st.tile([P, 512, 4], BF16, name="yg", align_bytes=64)
+                for k in range(2):
+                    h = slice(256 * k, 256 * k + 256)
+                    interleave4(yi[r][k], yg[:, h, :], y[:, :, h])
+                yc = st4.tile([P, 512], U32, name="yc", align_bytes=64)
+                nc.vector.quantize_mx(
+                    out=yc[:].bitcast(FP8X4), scales=ysc[:, r, :], in_=yg[:].rearrange("p n j -> p (n j)")
+                )
+                nc.sync.dma_start(
+                    out=out_1[a, :, m0 : m0 + 512, :].rearrange("p m j -> p (m j)").bitcast(I32), in_=yc[:].bitcast(I32)
+                )
+            o2 = out_2[a, :, :].rearrange("q (r g d) -> q r g d", r=R, g=G)
+            for q in range(4):
+                nc.sync.dma_start(
+                    out=o2[4 * q : 4 * q + 4, :, g, :].bitcast(I32), in_=ysc[32 * q : 32 * q + 4, :, :].bitcast(I32)
+                )
+
+        prep_w(1, 0, "vv")
+        stage_x(0, 0)
+        stage_1(0, 0, ((0, 1), (1, 1), (1, 2)), "ss")
+        stage_x(0, 1)
+        prep_w(2, 0, "sv")
+        stage_1(0, 1)
+        stage_2(0, 0)
+        prep_w(1, 1, "sv")
+        stage_x(1, 0)
+        stage_1(1, 0)
+        stage_2(0, 1)
+        prep_w(2, 1, "vv")
+        stage_x(1, 1)
+        stage_1(1, 1)
+        stage_2(1, 0)
+        stage_2(1, 1, ("vv", "sv"), ("ss", "vs"))

@@ -15,6 +15,33 @@ ALU = mybir.AluOpType
 ACT = mybir.ActivationFunctionType
 P = 128
 THR = 0.1
+UNITS = [(0, 0), (0, 1), (1, 0), (1, 1)]
+ORDER = """
+wint:1,0,0,V wint:1,0,1,V wq:1,0,0 wq:1,0,1 neg:1,0,V nq:1,0 x:0,0,0,S x:0,0,1,S
+xq:0,0 x:0,1,0,S x:0,1,1,S xq:0,1 wint:2,0,0,V l1:0,0,0,S l1:0,0,1,S wint:2,0,1,V
+l1:0,0,2,S wq:2,0,0 l1:0,0,3,S hint:0,0,V x:1,0,0,S x:1,0,1,S wq:2,0,1 hq:0,0
+neg:2,0,V nq:2,0 xq:1,0 x:1,1,0,S x:1,1,1,S l1:0,1,0,S l1:0,1,1,S l1:0,1,2,S
+xq:1,1 l1:0,1,3,S wint:1,1,0,V hint:0,1,V l1:1,0,0,S wint:1,1,1,S l1:1,0,1,S hq:0,1
+wq:1,1,0 l1:1,0,2,S x:2,0,0,S x:2,0,1,S wq:1,1,1 l1:1,0,3,S neg:1,1,V z:0,0,0
+wint:2,1,0,S nq:1,1 xq:2,0 hint:1,0,V l1:1,1,0,S x:2,1,0,S x:2,1,1,S z:0,0,1
+l1:1,1,1,S p:0,0,0,S hq:1,0 wint:2,1,1,V z:0,0,2 xq:2,1 wq:2,1,0 l1:1,1,2,S
+z:0,0,3 l1:1,1,3,S y:0,0,0 z:0,1,0 p:0,0,1,S wq:2,1,1 hint:1,1,V neg:2,1,S
+l1:2,0,0,S z:0,1,1 nq:2,1 x:3,0,0,S x:3,0,1,S l1:2,0,1,S p:0,1,0,S y:0,0,1
+sty:0,0 hq:1,1 z:0,1,2 l1:2,0,2,S xq:3,0 l1:2,0,3,S z:0,1,3 x:3,1,0,S
+x:3,1,1,S yint:0,0,0,S y:0,1,0 p:0,1,1,S yint:0,0,1,S z:1,0,0 hint:2,0,V l1:2,1,0,S
+xq:3,1 z:1,0,1 l1:2,1,1,S hq:2,0 p:1,0,0,S l1:2,1,2,S y:0,1,1 sty:0,1
+z:1,0,2 l1:2,1,3,S yq:0,0 z:1,0,3 yint:0,1,0,S z:1,1,0 hint:2,1,V yint:0,1,1,S
+y:1,0,0 p:1,0,1,S l1:3,0,0,S z:1,1,1 hq:2,1 l1:3,0,1,S p:1,1,0,S z:1,1,2
+y:1,0,1 sty:1,0 l1:3,0,2,S z:2,0,0 yq:0,1 z:1,1,3 l1:3,0,3,S y:1,1,0
+yint:1,0,0,S p:1,1,1,S z:2,0,1 yint:1,0,1,S l1:3,1,0,S hint:3,0,V p:2,0,0,S z:2,0,2
+l1:3,1,1,S hq:3,0 y:1,1,1 sty:1,1 l1:3,1,2,S z:2,0,3 y:2,0,0 p:2,0,1,S
+z:2,1,0 l1:3,1,3,S yq:1,0 yint:1,1,0,S yint:1,1,1,S z:2,1,1 hint:3,1,V p:2,1,0,S
+y:2,0,1 sty:2,0 z:2,1,2 hq:3,1 z:2,1,3 yint:2,0,0,S y:2,1,0 yint:2,0,1,S
+yq:1,1 p:2,1,1,S z:3,0,0 z:3,0,1 p:3,0,0,S z:3,0,2 y:2,1,1 sty:2,1
+yq:2,0 z:3,0,3 z:3,1,0 yint:2,1,0,S p:3,0,1,S y:3,0,0 yint:2,1,1,S z:3,1,1
+p:3,1,0,S z:3,1,2 y:3,0,1 sty:3,0 z:3,1,3 p:3,1,1,S y:3,1,0 yq:2,1
+yint:3,0,0,S yint:3,0,1,S y:3,1,1 sty:3,1 yint:3,1,0,V yq:3,0 yint:3,1,1,S yq:3,1
+"""
 
 
 def tile_afnocomplexblockspectralmlp_x1_kernel(tc, x, w1, b1, w2, b2, out_0, out_1, out_2):
@@ -23,13 +50,15 @@ def tile_afnocomplexblockspectralmlp_x1_kernel(tc, x, w1, b1, w2, b2, out_0, out
         const = ctx.enter_context(tc.tile_pool(name="const", bufs=1))
         xin = ctx.enter_context(tc.tile_pool(name="xin", bufs=8))
         win = ctx.enter_context(tc.tile_pool(name="win", bufs=6))
-        wst = ctx.enter_context(tc.tile_pool(name="wst", bufs=2))
+        wst = ctx.enter_context(tc.tile_pool(name="wst", bufs=3))
+        wneg = ctx.enter_context(tc.tile_pool(name="wneg", bufs=1))
         st = ctx.enter_context(tc.tile_pool(name="st", bufs=2))
         st3 = ctx.enter_context(tc.tile_pool(name="st3", bufs=3))
         st4 = ctx.enter_context(tc.tile_pool(name="st4", bufs=4))
         ps_x = ctx.enter_context(tc.psum_pool(name="ps_x", bufs=2))
         ps_1 = ctx.enter_context(tc.psum_pool(name="ps_1", bufs=3))
         ps_2 = ctx.enter_context(tc.psum_pool(name="ps_2", bufs=3))
+        ctx.enter_context(tc.manual_schedule())
 
         ident = const.tile([P, P], F32, name="ident")
         make_identity(nc, ident[:])
@@ -43,94 +72,111 @@ def tile_afnocomplexblockspectralmlp_x1_kernel(tc, x, w1, b1, w2, b2, out_0, out
             nc.sync.dma_start(out=t_[:], in_=w[r, g, :, :].rearrange("(p j) c -> p j c", j=4))
             wraw[layer, r, g] = t_
 
-        def load_x(r, g, a):
+        def load_x(r, u):
+            g, a = UNITS[u]
             t_ = xin.tile([P, 4, 512], BF16, name="xraw")
             nc.sync.dma_start(out=t_[:], in_=x[r, g, 512 * a : 512 * a + 512, :].rearrange("(p t) k -> p t k", t=4))
-            xraw[r, g, a] = t_
+            xraw[u, r] = t_
 
         load_w(1, 0, 0)
-        load_x(0, 0, 0)
+        load_x(0, 0)
         load_w(1, 1, 0)
-        load_x(1, 0, 0)
+        load_x(1, 0)
         b1b = const.tile([P, 4, 4], BF16, name="b1b")
         nc.sync.dma_start(out=b1b[:], in_=b1.rearrange("r g (p t) -> p (r g) t", t=4))
         load_w(2, 0, 0)
         load_w(2, 1, 0)
+        load_x(0, 1)
+        load_x(1, 1)
         b2b = const.tile([P, 2048], BF16, name="b2b")
         nc.sync.dma_start(out=b2b[:], in_=b2.rearrange("r g d -> (r g d)").partition_broadcast(P))
-        load_x(0, 0, 1)
-        load_x(1, 0, 1)
         load_w(1, 0, 1)
         load_w(1, 1, 1)
-        load_x(0, 1, 0)
-        load_x(1, 1, 0)
+        load_x(0, 2)
+        load_x(1, 2)
         load_w(2, 0, 1)
         load_w(2, 1, 1)
-        load_x(0, 1, 1)
-        load_x(1, 1, 1)
+        load_x(0, 3)
+        load_x(1, 3)
 
         b1f = const.tile([P, 16], F32, name="b1f")
-        nc.vector.tensor_copy(out=b1f[:], in_=b1b[:].rearrange("p a t -> p (a t)"))
+        nc.gpsimd.tensor_copy(out=b1f[:], in_=b1b[:].rearrange("p a t -> p (a t)"))
 
+        wgt = {}
+        wnt = {}
         wq = {}
+        xgt = {}
+        xq = {}
+        hrt = {}
+        hgt = {}
+        hq = {}
+        zt = {}
+        yt = {}
+        ygt = {}
+        sct = {}
 
         def quant(codes, scales, grouped):
             nc.vector.quantize_mx(
-                out=codes[:].bitcast(FP8X4), scales=scales[:], in_=grouped[:].rearrange("p n j -> p (n j)")
+                out=codes[:].bitcast(FP8X4), scales=scales, in_=grouped[:].rearrange("p n j -> p (n j)")
             )
 
-        def interleave4(eng, out, in_):
-            interleave(eng, out.rearrange("p (c i) t -> p c t i", i=4), in_.rearrange("p t (c i) -> p c t i", i=4))
-
-        def interleave(eng, out, in_):
-            if eng == "v":
+        def copy(eng, out, in_):
+            if eng == "V":
                 nc.vector.tensor_copy(out=out, in_=in_)
             else:
                 nc.scalar.copy(out=out, in_=in_)
 
-        def prep_w(layer, g, engs):
-            for r in range(2):
-                eng = engs[r]
-                raw = wraw[layer, r, g]
-                wg = wst.tile([P, 512, 4], BF16, name="wg", align_bytes=64)
-                if layer == 1:
-                    dst = wg[:].rearrange("p (t m) j -> p t m j", t=4)
-                    src = raw[:].rearrange("p j (m t) -> p t m j", t=4)
-                    interleave(eng, dst, src)
-                else:
-                    interleave4(eng, wg[:], raw[:])
-                c_ = const.tile([P, 512], U32, name="wc%d%d%d" % (layer, r, g), align_bytes=64)
-                s_ = const.tile([P, 512], U8, name="ws%d%d%d" % (layer, r, g), align_bytes=64)
-                quant(c_, s_, wg)
-                wq[layer, r, g] = (c_, s_)
-                if r == 1:
-                    wn = wst.tile([P, 512, 4], BF16, name="wn", align_bytes=64)
-                    nc.vector.tensor_scalar_mul(out=wn[:], in0=wg[:], scalar1=-1.0)
-                    c_ = const.tile([P, 512], U32, name="wcn%d%d" % (layer, g), align_bytes=64)
-                    s_ = const.tile([P, 512], U8, name="wsn%d%d" % (layer, g), align_bytes=64)
-                    quant(c_, s_, wn)
-                    wq[layer, 2, g] = (c_, s_)
+        def interleave4(eng, out, in_):
+            copy(eng, out.rearrange("p (c i) t -> p c t i", i=4), in_.rearrange("p t (c i) -> p c t i", i=4))
 
-        xq = {}
+        def wint(layer, g, r, eng):
+            raw = wraw[layer, r, g]
+            wg = wgt[layer, g, r] = wst.tile([P, 512, 4], BF16, name="wg", align_bytes=64)
+            if layer == 1:
+                copy(eng, wg[:].rearrange("p (t m) j -> p m j t", t=4), raw[:].rearrange("p j (m t) -> p m j t", t=4))
+            else:
+                interleave4(eng, wg[:], raw[:])
 
-        def stage_x(g, a):
-            for r in range(2):
-                words = xraw[r, g, a][:].bitcast(F32)
+        def wq_(layer, g, r):
+            c_ = const.tile([P, 512], U32, name="wc%d%d%d" % (layer, r, g), align_bytes=64)
+            s_ = const.tile([P, 512], U8, name="ws%d%d%d" % (layer, r, g), align_bytes=64)
+            quant(c_, s_[:], wgt[layer, g, r])
+            wq[layer, r, g] = (c_, s_)
+
+        def neg(layer, g, eng):
+            wn = wnt[layer, g] = wneg.tile([P, 512, 4], BF16, name="wn", align_bytes=64)
+            if eng == "V":
+                nc.vector.tensor_scalar_mul(out=wn[:], in0=wgt[layer, g, 1][:], scalar1=-1.0)
+            else:
+                nc.scalar.mul(out=wn[:], in_=wgt[layer, g, 1][:], mul=-1.0)
+
+        def nq(layer, g):
+            c_ = const.tile([P, 512], U32, name="wcn%d%d" % (layer, g), align_bytes=64)
+            s_ = const.tile([P, 512], U8, name="wsn%d%d" % (layer, g), align_bytes=64)
+            quant(c_, s_[:], wnt[layer, g])
+            wq[layer, 2, g] = (c_, s_)
+
+        def x_(u, r, h, eng):
+            words = xraw[u, r][:].bitcast(F32)
+            if (u, r) not in xgt:
                 xg = st.tile([P, 512, 4], BF16, name="xg", align_bytes=64)
-                xgw = xg[:].bitcast(F32)
-                for h in range(2):
-                    xt = ps_x.tile([P, 2, 2, P], F32, name="xt")
-                    for b in range(2):
-                        for u in range(2):
-                            nc.tensor.transpose(xt[:, b, u, :], words[:, 2 * h + b, u:256:2], ident[:])
-                    nc.scalar.copy(
-                        out=xgw[:, 256 * h : 256 * h + 256, :].rearrange("p (b n) u -> p b n u", b=2),
-                        in_=xt[:].rearrange("p b u n -> p b n u"),
-                    )
-                c_ = st4.tile([P, 512], U32, name="xc", align_bytes=64)
-                s_ = st4.tile([P, 512], U8, name="xs", align_bytes=64)
-                quant(c_, s_, xg)
-                xq[r, g, a] = (c_, s_)
+                xgt[u, r] = xg
+            xgw = xgt[u, r][:].bitcast(F32)
+            xt = ps_x.tile([P, 2, 2, P], F32, name="xt")
+            for b in range(2):
+                for k in range(2):
+                    nc.tensor.transpose(xt[:, b, k, :], words[:, 2 * h + b, k:256:2], ident[:])
+            copy(
+                eng,
+                xgw[:, 256 * h : 256 * h + 256, :].rearrange("p (b n) k -> p b n k", b=2),
+                xt[:].rearrange("p b k n -> p b n k"),
+            )
+
+        def xq_(u, r):
+            c_ = st4.tile([P, 512], U32, name="xc", align_bytes=64)
+            s_ = st4.tile([P, 512], U8, name="xs", align_bytes=64)
+            quant(c_, s_[:], xgt[u, r])
+            xq[u, r] = (c_, s_)
 
         def mm(out, lhs, lcols, rhs, first, last):
             nc.tensor.matmul_mx(
@@ -143,88 +189,101 @@ def tile_afnocomplexblockspectralmlp_x1_kernel(tc, x, w1, b1, w2, b2, out_0, out
                 stop=last,
             )
 
-        hq = {}
-
-        def stage_1(g, a, on_v=(), hint="vs"):
-            for r in range(2):
+        def l1(u, r, t, eng):
+            g = UNITS[u][0]
+            if (u, r) not in hrt:
                 hraw = st3.tile([P, 4, 512], BF16, name="hraw")
-                wa, wb = ((1, 0, g), (1, 2, g)) if r == 0 else ((1, 1, g), (1, 0, g))
-                for t in range(4):
-                    cols = slice(P * t, P * t + P)
-                    acc = ps_1.tile([P, 512], F32, name="acc1")
-                    mm(acc[:], wq[wa], cols, xq[0, g, a], True, False)
-                    mm(acc[:], wq[wb], cols, xq[1, g, a], False, True)
-                    i = (r * G + g) * 4 + t
-                    if (r, t) in on_v:
-                        nc.vector.tensor_scalar(
-                            out=hraw[:, t, :], in0=acc[:], scalar1=b1f[:, i : i + 1], scalar2=0.0, op0=ALU.add, op1=ALU.max
-                        )
-                    else:
-                        nc.scalar.activation(out=hraw[:, t, :], in_=acc[:], func=ACT.Relu, bias=b1f[:, i : i + 1])
-                hg = st.tile([P, 512, 4], BF16, name="hg", align_bytes=64)
-                interleave4(hint[r], hg[:], hraw[:])
-                c_ = st4.tile([P, 512], U32, name="hc", align_bytes=64)
-                s_ = st4.tile([P, 512], U8, name="hs", align_bytes=64)
-                quant(c_, s_, hg)
-                hq[r, g, a] = (c_, s_)
+                hrt[u, r] = hraw
+            wa, wb = ((1, 0, g), (1, 2, g)) if r == 0 else ((1, 1, g), (1, 0, g))
+            cols = slice(P * t, P * t + P)
+            acc = ps_1.tile([P, 512], F32, name="acc1")
+            mm(acc[:], wq[wa], cols, xq[u, 0], True, False)
+            mm(acc[:], wq[wb], cols, xq[u, 1], False, True)
+            i = (r * G + g) * 4 + t
+            if eng == "V":
+                nc.vector.tensor_scalar(
+                    out=hrt[u, r][:, t, :], in0=acc[:], scalar1=b1f[:, i : i + 1], scalar2=0.0, op0=ALU.add, op1=ALU.max
+                )
+            else:
+                nc.scalar.activation(out=hrt[u, r][:, t, :], in_=acc[:], func=ACT.Relu, bias=b1f[:, i : i + 1])
 
-        def stage_2(g, a, p_eng=("vv", "ss"), yi=("ss", "ss")):
-            ysc = st4.tile([P, 2, 512], U8, name="ysc", align_bytes=64)
-            for r in range(2):
-                wa, wb = ((2, 0, g), (2, 2, g)) if r == 0 else ((2, 1, g), (2, 0, g))
+        def hint(u, r, eng):
+            hg = hgt[u, r] = st.tile([P, 512, 4], BF16, name="hg", align_bytes=64)
+            interleave4(eng, hg[:], hrt[u, r][:])
+
+        def hq_(u, r):
+            c_ = st4.tile([P, 512], U32, name="hc", align_bytes=64)
+            s_ = st4.tile([P, 512], U8, name="hs", align_bytes=64)
+            quant(c_, s_[:], hgt[u, r])
+            hq[u, r] = (c_, s_)
+
+        def z_(u, r, t):
+            g = UNITS[u][0]
+            if (u, r) not in zt:
                 z = st3.tile([P, 4, 512], F32, name="z")
                 y = st4.tile([P, 4, 512], F32, name="y")
-                m0 = (r * G + g) * 512
-                for t in range(4):
-                    cols = slice(P * t, P * t + P)
-                    acc = ps_2.tile([P, 512], F32, name="acc2")
-                    mm(acc[:], hq[0, g, a], cols, wq[wa], True, False)
-                    mm(acc[:], hq[1, g, a], cols, wq[wb], False, True)
-                    nc.vector.tensor_tensor(out=z[:, t, :], in0=acc[:], in1=b2b[:, m0 : m0 + 512], op=ALU.add)
-                    if t % 2 == 1:
-                        h = slice(t - 1, t + 1)
-                        if p_eng[r][t // 2] == "v":
-                            nc.vector.tensor_scalar(
-                                out=y[:, h, :], in0=z[:, h, :], scalar1=-THR, scalar2=0.0, op0=ALU.add, op1=ALU.max
-                            )
-                        else:
-                            nc.scalar.activation(out=y[:, h, :], in_=z[:, h, :], func=ACT.Relu, bias=-THR)
-                        nc.vector.scalar_tensor_tensor(
-                            out=y[:, h, :], in0=z[:, h, :], scalar=THR, in1=y[:, h, :], op0=ALU.add, op1=ALU.min
-                        )
-                nc.sync.dma_start(
-                    out=out_0[r, g, 512 * a : 512 * a + 512, :].rearrange("(p t) d -> p t d", t=4), in_=y[:]
-                )
-                yg = st.tile([P, 512, 4], BF16, name="yg", align_bytes=64)
-                for k in range(2):
-                    h = slice(256 * k, 256 * k + 256)
-                    interleave4(yi[r][k], yg[:, h, :], y[:, :, h])
-                yc = st4.tile([P, 512], U32, name="yc", align_bytes=64)
-                nc.vector.quantize_mx(
-                    out=yc[:].bitcast(FP8X4), scales=ysc[:, r, :], in_=yg[:].rearrange("p n j -> p (n j)")
-                )
-                nc.sync.dma_start(
-                    out=out_1[a, :, m0 : m0 + 512, :].rearrange("p m j -> p (m j)").bitcast(I32), in_=yc[:].bitcast(I32)
-                )
-            o2 = out_2[a, :, :].rearrange("q (r g d) -> q r g d", r=R, g=G)
-            for q in range(4):
-                nc.sync.dma_start(
-                    out=o2[4 * q : 4 * q + 4, :, g, :].bitcast(I32), in_=ysc[32 * q : 32 * q + 4, :, :].bitcast(I32)
-                )
+                zt[u, r] = z
+                yt[u, r] = y
+            wa, wb = ((2, 0, g), (2, 2, g)) if r == 0 else ((2, 1, g), (2, 0, g))
+            m0 = (r * G + g) * 512
+            cols = slice(P * t, P * t + P)
+            acc = ps_2.tile([P, 512], F32, name="acc2")
+            mm(acc[:], hq[u, 0], cols, wq[wa], True, False)
+            mm(acc[:], hq[u, 1], cols, wq[wb], False, True)
+            nc.vector.tensor_tensor(out=zt[u, r][:, t, :], in0=acc[:], in1=b2b[:, m0 : m0 + 512], op=ALU.add)
 
-        prep_w(1, 0, "vv")
-        stage_x(0, 0)
-        stage_1(0, 0, ((0, 1), (1, 1), (1, 2)), "ss")
-        stage_x(0, 1)
-        prep_w(2, 0, "sv")
-        stage_1(0, 1)
-        stage_2(0, 0)
-        prep_w(1, 1, "sv")
-        stage_x(1, 0)
-        stage_1(1, 0)
-        stage_2(0, 1)
-        prep_w(2, 1, "vv")
-        stage_x(1, 1)
-        stage_1(1, 1)
-        stage_2(1, 0)
-        stage_2(1, 1, ("vv", "sv"), ("ss", "vs"))
+        def p_(u, r, k, eng):
+            h = slice(2 * k, 2 * k + 2)
+            if eng == "V":
+                nc.vector.tensor_scalar(
+                    out=yt[u, r][:, h, :], in0=zt[u, r][:, h, :], scalar1=-THR, scalar2=0.0, op0=ALU.add, op1=ALU.max
+                )
+            else:
+                nc.scalar.activation(out=yt[u, r][:, h, :], in_=zt[u, r][:, h, :], func=ACT.Relu, bias=-THR)
+
+        def y_(u, r, k):
+            h = slice(2 * k, 2 * k + 2)
+            y = yt[u, r]
+            nc.vector.scalar_tensor_tensor(
+                out=y[:, h, :], in0=zt[u, r][:, h, :], scalar=THR, in1=y[:, h, :], op0=ALU.add, op1=ALU.min
+            )
+
+        def sty(u, r):
+            g, a = UNITS[u]
+            nc.sync.dma_start(
+                out=out_0[r, g, 512 * a : 512 * a + 512, :].rearrange("(p t) d -> p t d", t=4), in_=yt[u, r][:]
+            )
+
+        def yint(u, r, k, eng):
+            if (u, r) not in ygt:
+                yg = st.tile([P, 512, 4], BF16, name="yg", align_bytes=64)
+                ygt[u, r] = yg
+            h = slice(256 * k, 256 * k + 256)
+            interleave4(eng, ygt[u, r][:, h, :], yt[u, r][:, :, h])
+
+        def yq(u, r):
+            g, a = UNITS[u]
+            m0 = (r * G + g) * 512
+            if u not in sct:
+                ysc = st4.tile([P, 2, 512], U8, name="ysc", align_bytes=64)
+                sct[u] = [ysc, 0]
+            yc = st4.tile([P, 512], U32, name="yc", align_bytes=64)
+            quant(yc, sct[u][0][:, r, :], ygt[u, r])
+            nc.sync.dma_start(
+                out=out_1[a, :, m0 : m0 + 512, :].rearrange("p m j -> p (m j)").bitcast(I32), in_=yc[:].bitcast(I32)
+            )
+            sct[u][1] += 1
+            if sct[u][1] == 2:
+                o2 = out_2[a, :, :].rearrange("q (r g d) -> q r g d", r=R, g=G)
+                for q in range(4):
+                    nc.sync.dma_start(
+                        out=o2[4 * q : 4 * q + 4, :, g, :].bitcast(I32),
+                        in_=sct[u][0][32 * q : 32 * q + 4, :, :].bitcast(I32),
+                    )
+
+        steps = {"wint": wint, "wq": wq_, "neg": neg, "nq": nq, "x": x_, "xq": xq_, "l1": l1, "hint": hint, "hq": hq_,
+                 "z": z_, "p": p_, "y": y_, "sty": sty, "yint": yint, "yq": yq}
+        for word in ORDER.split():
+            parts = word.split(":")
+            args = [s if s in ("V", "S") else int(s) for s in parts[1].split(",")]
+            steps[parts[0]](*args)

@@ -17,30 +17,30 @@ P = 128
 THR = 0.1
 UNITS = [(0, 0), (0, 1), (1, 0), (1, 1)]
 ORDER = """
-wint:1,0,0,V wint:1,0,1,V wq:1,0,0 wq:1,0,1 neg:1,0,V nq:1,0 x:0,0,0,S x:0,0,1,S
-xq:0,0 x:0,1,0,S x:0,1,1,S xq:0,1 wint:2,0,0,V l1:0,0,0,S l1:0,0,1,S wint:2,0,1,V
-l1:0,0,2,S wq:2,0,0 l1:0,0,3,S hint:0,0,V x:1,0,0,S x:1,0,1,S wq:2,0,1 hq:0,0
-neg:2,0,V nq:2,0 xq:1,0 x:1,1,0,S x:1,1,1,S l1:0,1,0,S l1:0,1,1,S l1:0,1,2,S
-xq:1,1 l1:0,1,3,S wint:1,1,0,V hint:0,1,V l1:1,0,0,S wint:1,1,1,S l1:1,0,1,S hq:0,1
-wq:1,1,0 l1:1,0,2,S x:2,0,0,S x:2,0,1,S wq:1,1,1 l1:1,0,3,S neg:1,1,V z:0,0,0
-wint:2,1,0,S nq:1,1 xq:2,0 hint:1,0,V l1:1,1,0,S x:2,1,0,S x:2,1,1,S z:0,0,1
-l1:1,1,1,S p:0,0,0,S hq:1,0 wint:2,1,1,V z:0,0,2 xq:2,1 wq:2,1,0 l1:1,1,2,S
-z:0,0,3 l1:1,1,3,S y:0,0,0 z:0,1,0 p:0,0,1,S wq:2,1,1 hint:1,1,V neg:2,1,S
-l1:2,0,0,S z:0,1,1 nq:2,1 x:3,0,0,S x:3,0,1,S l1:2,0,1,S p:0,1,0,S y:0,0,1
-sty:0,0 hq:1,1 z:0,1,2 l1:2,0,2,S xq:3,0 l1:2,0,3,S z:0,1,3 x:3,1,0,S
-x:3,1,1,S yint:0,0,0,S y:0,1,0 p:0,1,1,S yint:0,0,1,S z:1,0,0 hint:2,0,V l1:2,1,0,S
-xq:3,1 z:1,0,1 l1:2,1,1,S hq:2,0 p:1,0,0,S l1:2,1,2,S y:0,1,1 sty:0,1
-z:1,0,2 l1:2,1,3,S yq:0,0 z:1,0,3 yint:0,1,0,S z:1,1,0 hint:2,1,V yint:0,1,1,S
-y:1,0,0 p:1,0,1,S l1:3,0,0,S z:1,1,1 hq:2,1 l1:3,0,1,S p:1,1,0,S z:1,1,2
-y:1,0,1 sty:1,0 l1:3,0,2,S z:2,0,0 yq:0,1 z:1,1,3 l1:3,0,3,S y:1,1,0
-yint:1,0,0,S p:1,1,1,S z:2,0,1 yint:1,0,1,S l1:3,1,0,S hint:3,0,V p:2,0,0,S z:2,0,2
-l1:3,1,1,S hq:3,0 y:1,1,1 sty:1,1 l1:3,1,2,S z:2,0,3 y:2,0,0 p:2,0,1,S
-z:2,1,0 l1:3,1,3,S yq:1,0 yint:1,1,0,S yint:1,1,1,S z:2,1,1 hint:3,1,V p:2,1,0,S
-y:2,0,1 sty:2,0 z:2,1,2 hq:3,1 z:2,1,3 yint:2,0,0,S y:2,1,0 yint:2,0,1,S
-yq:1,1 p:2,1,1,S z:3,0,0 z:3,0,1 p:3,0,0,S z:3,0,2 y:2,1,1 sty:2,1
-yq:2,0 z:3,0,3 z:3,1,0 yint:2,1,0,S p:3,0,1,S y:3,0,0 yint:2,1,1,S z:3,1,1
-p:3,1,0,S z:3,1,2 y:3,0,1 sty:3,0 z:3,1,3 p:3,1,1,S y:3,1,0 yq:2,1
-yint:3,0,0,S yint:3,0,1,S y:3,1,1 sty:3,1 yint:3,1,0,V yq:3,0 yint:3,1,1,S yq:3,1
+wint:1,0,0,V wq:1,0,0 wint:1,0,1,V wq:1,0,1 neg:1,0,V nq:1,0 x:0,0,0,S x:0,0,1,S
+xq:0,0 x:0,1,0,V x:0,1,1,V wint:2,0,0,S xq:0,1 wq:2,0,0 wint:2,0,1,V wq:2,0,1
+x:1,0,0,S x:1,0,1,S xq:1,0 l1:0,0,0,S x:1,1,0,S x:1,1,1,S l1:0,0,1,S l1:0,0,2,S
+neg:2,0,V l1:0,0,3,S l1:0,1,0,S xq:1,1 l1:0,1,1,S l1:0,1,2,S l1:0,1,3,S nq:2,0
+hint:0,0,V wint:1,1,0,V l1:1,0,0,S hint:0,1,V l1:1,0,1,S x:2,0,0,S wq:1,1,0 hq:0,0
+wint:1,1,1,V x:2,0,1,S l1:1,0,2,S xq:2,0 hq:0,1 wq:1,1,1 l1:1,0,3,S x:2,1,0,S
+x:2,1,1,S l1:1,1,0,S xq:2,1 z:0,0,0 hint:1,0,S l1:1,1,1,S neg:1,1,V z:0,0,1
+l1:1,1,2,S hq:1,0 z:0,0,2 nq:1,1 l1:1,1,3,S z:0,0,3 p:0,0,0,S z:0,1,0
+hint:1,1,S z:0,1,1 x:3,0,0,S p:0,0,1,V x:3,0,1,S y:0,0,0 wint:2,1,0,V l1:2,0,0,S
+z:0,1,2 hq:1,1 l1:2,0,1,S xq:3,0 l1:2,0,2,S z:0,1,3 l1:2,0,3,S wq:2,1,0
+wint:2,1,1,V x:3,1,0,S p:0,1,0,V y:0,0,1 sty:0,0 x:3,1,1,S xq:3,1 wq:2,1,1
+hint:2,0,S l1:2,1,0,S p:0,1,1,S l1:2,1,1,S y:0,1,0 l1:2,1,2,S z:1,0,0 l1:2,1,3,S
+hq:2,0 z:1,0,1 y:0,1,1 sty:0,1 neg:2,1,V hint:2,1,S z:1,0,2 yint:0,0,0,S
+z:1,1,0 nq:2,1 l1:3,0,0,S yint:0,0,1,S z:1,0,3 p:1,0,0,S hq:2,1 l1:3,0,1,S
+z:1,1,1 l1:3,0,2,S z:1,1,2 z:2,0,0 p:1,0,1,V y:1,0,0 l1:3,0,3,S z:1,1,3
+p:1,1,0,V yq:0,0 z:2,0,1 yint:0,1,0,S yint:0,1,1,S y:1,0,1 sty:1,0 hint:3,0,S
+l1:3,1,0,S z:2,0,2 p:1,1,1,S y:1,1,0 l1:3,1,1,S p:2,0,0,S z:2,1,0 z:2,0,3
+hq:3,0 l1:3,1,2,S z:2,1,1 yq:0,1 y:1,1,1 sty:1,1 l1:3,1,3,S y:2,0,0
+p:2,0,1,V z:2,1,2 hint:3,1,S p:2,1,0,V yint:1,0,0,S z:2,1,3 yint:1,0,1,S y:2,0,1
+sty:2,0 hq:3,1 y:2,1,0 p:2,1,1,S yint:1,1,0,S yint:1,1,1,S z:3,0,0 yq:1,0
+z:3,0,1 z:3,0,2 y:2,1,1 sty:2,1 z:3,0,3 z:3,1,0 yint:2,0,0,S p:3,0,0,S
+yint:2,0,1,S z:3,1,1 yq:1,1 z:3,1,2 p:3,0,1,S z:3,1,3 y:3,0,0 p:3,1,0,S
+y:3,0,1 sty:3,0 p:3,1,1,S yint:2,1,0,S yq:2,0 yint:2,1,1,S y:3,1,0 y:3,1,1
+sty:3,1 yq:2,1 yint:3,0,0,V yint:3,0,1,S yint:3,1,0,V yint:3,1,1,S yq:3,0 yq:3,1
 """
 
 
@@ -78,18 +78,23 @@ def tile_afnocomplexblockspectralmlp_x1_kernel(tc, x, w1, b1, w2, b2, out_0, out
             nc.sync.dma_start(out=t_[:], in_=x[r, g, 512 * a : 512 * a + 512, :].rearrange("(p t) k -> p t k", t=4))
             xraw[u, r] = t_
 
+        b1b = const.tile([P, 4, 4], BF16, name="b1b")
+        nc.scalar.dma_start(out=b1b[:], in_=b1.rearrange("r g (p t) -> p (r g) t", t=4))
         load_w(1, 0, 0)
         load_x(0, 0)
         load_w(1, 1, 0)
         load_x(1, 0)
-        b1b = const.tile([P, 4, 4], BF16, name="b1b")
-        nc.sync.dma_start(out=b1b[:], in_=b1.rearrange("r g (p t) -> p (r g) t", t=4))
         load_w(2, 0, 0)
         load_w(2, 1, 0)
         load_x(0, 1)
         load_x(1, 1)
-        b2b = const.tile([P, 2048], BF16, name="b2b")
-        nc.sync.dma_start(out=b2b[:], in_=b2.rearrange("r g d -> (r g d)").partition_broadcast(P))
+        b2b = const.tile([P, 2, 2, 512], BF16, name="b2b")
+
+        def load_b2(g):
+            for r in range(2):
+                nc.sync.dma_start(out=b2b[:, r, g, :], in_=b2[r, g, :].partition_broadcast(P))
+
+        load_b2(0)
         load_w(1, 0, 1)
         load_w(1, 1, 1)
         load_x(0, 2)
@@ -98,6 +103,7 @@ def tile_afnocomplexblockspectralmlp_x1_kernel(tc, x, w1, b1, w2, b2, out_0, out
         load_w(2, 1, 1)
         load_x(0, 3)
         load_x(1, 3)
+        load_b2(1)
 
         b1f = const.tile([P, 16], F32, name="b1f")
         nc.gpsimd.tensor_copy(out=b1f[:], in_=b1b[:].rearrange("p a t -> p (a t)"))
@@ -123,6 +129,8 @@ def tile_afnocomplexblockspectralmlp_x1_kernel(tc, x, w1, b1, w2, b2, out_0, out
         def copy(eng, out, in_):
             if eng == "V":
                 nc.vector.tensor_copy(out=out, in_=in_)
+            elif eng == "G":
+                nc.gpsimd.tensor_scalar(out=out, in0=in_, scalar1=1.0, scalar2=0.0, op0=ALU.mult, op1=ALU.add)
             else:
                 nc.scalar.copy(out=out, in_=in_)
 
@@ -135,7 +143,10 @@ def tile_afnocomplexblockspectralmlp_x1_kernel(tc, x, w1, b1, w2, b2, out_0, out
             if layer == 1:
                 copy(eng, wg[:].rearrange("p (t m) j -> p m j t", t=4), raw[:].rearrange("p j (m t) -> p m j t", t=4))
             else:
-                interleave4(eng, wg[:], raw[:])
+                if eng == "G":
+                    copy(eng, wg[:], raw[:].rearrange("p j c -> p c j"))
+                else:
+                    interleave4(eng, wg[:], raw[:])
 
         def wq_(layer, g, r):
             c_ = const.tile([P, 512], U32, name="wc%d%d%d" % (layer, r, g), align_bytes=64)
@@ -230,12 +241,13 @@ def tile_afnocomplexblockspectralmlp_x1_kernel(tc, x, w1, b1, w2, b2, out_0, out
             acc = ps_2.tile([P, 512], F32, name="acc2")
             mm(acc[:], hq[u, 0], cols, wq[wa], True, False)
             mm(acc[:], hq[u, 1], cols, wq[wb], False, True)
-            nc.vector.tensor_tensor(out=zt[u, r][:, t, :], in0=acc[:], in1=b2b[:, m0 : m0 + 512], op=ALU.add)
+            nc.vector.tensor_tensor(out=zt[u, r][:, t, :], in0=acc[:], in1=b2b[:, r, g, :], op=ALU.add)
 
         def p_(u, r, k, eng):
             h = slice(2 * k, 2 * k + 2)
-            if eng == "V":
-                nc.vector.tensor_scalar(
+            if eng in "VG":
+                e = nc.vector if eng == "V" else nc.gpsimd
+                e.tensor_scalar(
                     out=yt[u, r][:, h, :], in0=zt[u, r][:, h, :], scalar1=-THR, scalar2=0.0, op0=ALU.add, op1=ALU.max
                 )
             else:
@@ -259,7 +271,10 @@ def tile_afnocomplexblockspectralmlp_x1_kernel(tc, x, w1, b1, w2, b2, out_0, out
                 yg = st.tile([P, 512, 4], BF16, name="yg", align_bytes=64)
                 ygt[u, r] = yg
             h = slice(256 * k, 256 * k + 256)
-            interleave4(eng, ygt[u, r][:, h, :], yt[u, r][:, :, h])
+            if eng == "G":
+                copy(eng, ygt[u, r][:, h, :], yt[u, r][:, :, h].rearrange("p t d -> p d t"))
+            else:
+                interleave4(eng, ygt[u, r][:, h, :], yt[u, r][:, :, h])
 
         def yq(u, r):
             g, a = UNITS[u]
@@ -276,7 +291,8 @@ def tile_afnocomplexblockspectralmlp_x1_kernel(tc, x, w1, b1, w2, b2, out_0, out
             if sct[u][1] == 2:
                 o2 = out_2[a, :, :].rearrange("q (r g d) -> q r g d", r=R, g=G)
                 for q in range(4):
-                    nc.sync.dma_start(
+                    eng = nc.scalar if u == 3 and q % 2 else nc.sync
+                    eng.dma_start(
                         out=o2[4 * q : 4 * q + 4, :, g, :].bitcast(I32),
                         in_=sct[u][0][32 * q : 32 * q + 4, :, :].bitcast(I32),
                     )
@@ -285,5 +301,5 @@ def tile_afnocomplexblockspectralmlp_x1_kernel(tc, x, w1, b1, w2, b2, out_0, out
                  "z": z_, "p": p_, "y": y_, "sty": sty, "yint": yint, "yq": yq}
         for word in ORDER.split():
             parts = word.split(":")
-            args = [s if s in ("V", "S") else int(s) for s in parts[1].split(",")]
+            args = [s if s in ("V", "S", "G") else int(s) for s in parts[1].split(",")]
             steps[parts[0]](*args)

from contextlib import ExitStack

import concourse.mybir as mybir
from concourse.masks import make_identity

R, G, T, D, F = 2, 2, 1024, 512, 512
FLOPS = 2 * 8 * G * T * D * F
F32 = mybir.dt.float32
BF16 = mybir.dt.bfloat16
U32 = mybir.dt.uint32
I32 = mybir.dt.int32
U8 = mybir.dt.uint8
FP8X4 = mybir.dt.float8_e4m3fn_x4
ALU = mybir.AluOpType
ACT = mybir.ActivationFunctionType
P = 128
THR = 0.1
UNITS = [(0, 0), (0, 1), (1, 0), (1, 1)]
ORDER = """
wint:1,0,0,V wq:1,0,0 wint:1,0,1,V wq:1,0,1 neg:1,0,V nq:1,0 x:0,0,0,S x:0,0,1,S
xq:0,0 x:0,1,0,V x:0,1,1,V wint:2,0,0,S xq:0,1 wq:2,0,0 wint:2,0,1,V wq:2,0,1
x:1,0,0,S x:1,0,1,S xq:1,0 l1:0,0,0,S x:1,1,0,S x:1,1,1,S l1:0,0,1,S l1:0,0,2,S
neg:2,0,V l1:0,0,3,S l1:0,1,0,S xq:1,1 l1:0,1,1,S l1:0,1,2,S l1:0,1,3,S nq:2,0
hint:0,0,V wint:1,1,0,V l1:1,0,0,S hint:0,1,V l1:1,0,1,S x:2,0,0,S wq:1,1,0 hq:0,0
wint:1,1,1,V x:2,0,1,S l1:1,0,2,S xq:2,0 hq:0,1 wq:1,1,1 l1:1,0,3,S x:2,1,0,S
x:2,1,1,S l1:1,1,0,S xq:2,1 z:0,0,0 hint:1,0,S l1:1,1,1,S neg:1,1,V z:0,0,1
l1:1,1,2,S hq:1,0 z:0,0,2 nq:1,1 l1:1,1,3,S z:0,0,3 p:0,0,0,S z:0,1,0
hint:1,1,S z:0,1,1 x:3,0,0,S p:0,0,1,V x:3,0,1,S y:0,0,0 wint:2,1,0,V l1:2,0,0,S
z:0,1,2 hq:1,1 l1:2,0,1,S xq:3,0 l1:2,0,2,S z:0,1,3 l1:2,0,3,S wq:2,1,0
wint:2,1,1,V x:3,1,0,S p:0,1,0,V y:0,0,1 sty:0,0 x:3,1,1,S xq:3,1 wq:2,1,1
hint:2,0,S l1:2,1,0,S p:0,1,1,S l1:2,1,1,S y:0,1,0 l1:2,1,2,S z:1,0,0 l1:2,1,3,S
hq:2,0 z:1,0,1 y:0,1,1 sty:0,1 neg:2,1,V hint:2,1,S z:1,0,2 yint:0,0,0,S
z:1,1,0 nq:2,1 l1:3,0,0,S yint:0,0,1,S z:1,0,3 p:1,0,0,S hq:2,1 l1:3,0,1,S
z:1,1,1 l1:3,0,2,S z:1,1,2 z:2,0,0 p:1,0,1,V y:1,0,0 l1:3,0,3,S z:1,1,3
p:1,1,0,V yq:0,0 z:2,0,1 yint:0,1,0,S yint:0,1,1,S y:1,0,1 sty:1,0 hint:3,0,S
l1:3,1,0,S z:2,0,2 p:1,1,1,S y:1,1,0 l1:3,1,1,S p:2,0,0,S z:2,1,0 z:2,0,3
hq:3,0 l1:3,1,2,S z:2,1,1 yq:0,1 y:1,1,1 sty:1,1 l1:3,1,3,S y:2,0,0
p:2,0,1,V z:2,1,2 hint:3,1,S p:2,1,0,V yint:1,0,0,S z:2,1,3 yint:1,0,1,S y:2,0,1
sty:2,0 hq:3,1 y:2,1,0 p:2,1,1,S yint:1,1,0,S yint:1,1,1,S z:3,0,0 yq:1,0
z:3,0,1 z:3,0,2 y:2,1,1 sty:2,1 z:3,0,3 z:3,1,0 yint:2,0,0,S p:3,0,0,S
yint:2,0,1,S z:3,1,1 yq:1,1 z:3,1,2 p:3,0,1,S z:3,1,3 y:3,0,0 p:3,1,0,S
y:3,0,1 sty:3,0 p:3,1,1,S yint:2,1,0,S yq:2,0 yint:2,1,1,S y:3,1,0 y:3,1,1
sty:3,1 yq:2,1 yint:3,0,0,V yint:3,0,1,S yint:3,1,0,V yint:3,1,1,S yq:3,0 yq:3,1
"""


def tile_afnocomplexblockspectralmlp_x1_kernel(tc, x, w1, b1, w2, b2, out_0, out_1, out_2):
    nc = tc.nc
    with ExitStack() as ctx:
        const = ctx.enter_context(tc.tile_pool(name="const", bufs=1))
        xin = ctx.enter_context(tc.tile_pool(name="xin", bufs=8))
        win = ctx.enter_context(tc.tile_pool(name="win", bufs=6))
        wst = ctx.enter_context(tc.tile_pool(name="wst", bufs=3))
        wneg = ctx.enter_context(tc.tile_pool(name="wneg", bufs=1))
        st = ctx.enter_context(tc.tile_pool(name="st", bufs=2))
        st3 = ctx.enter_context(tc.tile_pool(name="st3", bufs=3))
        st4 = ctx.enter_context(tc.tile_pool(name="st4", bufs=4))
        ps_x = ctx.enter_context(tc.psum_pool(name="ps_x", bufs=2))
        ps_1 = ctx.enter_context(tc.psum_pool(name="ps_1", bufs=3))
        ps_2 = ctx.enter_context(tc.psum_pool(name="ps_2", bufs=3))
        ctx.enter_context(tc.manual_schedule())

        ident = const.tile([P, P], F32, name="ident")
        make_identity(nc, ident[:])

        wraw = {}
        xraw = {}

        def load_w(layer, r, g):
            w = w1 if layer == 1 else w2
            t_ = win.tile([P, 4, 512], BF16, name="wraw")
            nc.sync.dma_start(out=t_[:], in_=w[r, g, :, :].rearrange("(p j) c -> p j c", j=4))
            wraw[layer, r, g] = t_

        def load_x(r, u):
            g, a = UNITS[u]
            t_ = xin.tile([P, 4, 512], BF16, name="xraw")
            nc.sync.dma_start(out=t_[:], in_=x[r, g, 512 * a : 512 * a + 512, :].rearrange("(p t) k -> p t k", t=4))
            xraw[u, r] = t_

        b1b = const.tile([P, 4, 4], BF16, name="b1b")
        nc.scalar.dma_start(out=b1b[:], in_=b1.rearrange("r g (p t) -> p (r g) t", t=4))
        load_w(1, 0, 0)
        load_x(0, 0)
        load_w(1, 1, 0)
        load_x(1, 0)
        load_w(2, 0, 0)
        load_w(2, 1, 0)
        load_x(0, 1)
        load_x(1, 1)
        b2b = const.tile([P, 2, 2, 512], BF16, name="b2b")

        def load_b2(g):
            for r in range(2):
                nc.sync.dma_start(out=b2b[:, r, g, :], in_=b2[r, g, :].partition_broadcast(P))

        load_b2(0)
        load_w(1, 0, 1)
        load_w(1, 1, 1)
        load_x(0, 2)
        load_x(1, 2)
        load_w(2, 0, 1)
        load_w(2, 1, 1)
        load_x(0, 3)
        load_x(1, 3)
        load_b2(1)

        b1f = const.tile([P, 16], F32, name="b1f")
        nc.gpsimd.tensor_copy(out=b1f[:], in_=b1b[:].rearrange("p a t -> p (a t)"))

        wgt = {}
        wnt = {}
        wq = {}
        xgt = {}
        xq = {}
        hrt = {}
        hgt = {}
        hq = {}
        zt = {}
        yt = {}
        ygt = {}
        sct = {}

        def quant(codes, scales, grouped):
            nc.vector.quantize_mx(
                out=codes[:].bitcast(FP8X4), scales=scales, in_=grouped[:].rearrange("p n j -> p (n j)")
            )

        def copy(eng, out, in_):
            if eng == "V":
                nc.vector.tensor_copy(out=out, in_=in_)
            elif eng == "G":
                nc.gpsimd.tensor_scalar(out=out, in0=in_, scalar1=1.0, scalar2=0.0, op0=ALU.mult, op1=ALU.add)
            else:
                nc.scalar.copy(out=out, in_=in_)

        def interleave4(eng, out, in_):
            copy(eng, out.rearrange("p (c i) t -> p c t i", i=4), in_.rearrange("p t (c i) -> p c t i", i=4))

        def wint(layer, g, r, eng):
            raw = wraw[layer, r, g]
            wg = wgt[layer, g, r] = wst.tile([P, 512, 4], BF16, name="wg", align_bytes=64)
            if layer == 1:
                copy(eng, wg[:].rearrange("p (t m) j -> p m j t", t=4), raw[:].rearrange("p j (m t) -> p m j t", t=4))
            else:
                if eng == "G":
                    copy(eng, wg[:], raw[:].rearrange("p j c -> p c j"))
                else:
                    interleave4(eng, wg[:], raw[:])

        def wq_(layer, g, r):
            c_ = const.tile([P, 512], U32, name="wc%d%d%d" % (layer, r, g), align_bytes=64)
            s_ = const.tile([P, 512], U8, name="ws%d%d%d" % (layer, r, g), align_bytes=64)
            quant(c_, s_[:], wgt[layer, g, r])
            wq[layer, r, g] = (c_, s_)

        def neg(layer, g, eng):
            wn = wnt[layer, g] = wneg.tile([P, 512, 4], BF16, name="wn", align_bytes=64)
            if eng == "V":
                nc.vector.tensor_scalar_mul(out=wn[:], in0=wgt[layer, g, 1][:], scalar1=-1.0)
            else:
                nc.scalar.mul(out=wn[:], in_=wgt[layer, g, 1][:], mul=-1.0)

        def nq(layer, g):
            c_ = const.tile([P, 512], U32, name="wcn%d%d" % (layer, g), align_bytes=64)
            s_ = const.tile([P, 512], U8, name="wsn%d%d" % (layer, g), align_bytes=64)
            quant(c_, s_[:], wnt[layer, g])
            wq[layer, 2, g] = (c_, s_)

        def x_(u, r, h, eng):
            words = xraw[u, r][:].bitcast(F32)
            if (u, r) not in xgt:
                xg = st.tile([P, 512, 4], BF16, name="xg", align_bytes=64)
                xgt[u, r] = xg
            xgw = xgt[u, r][:].bitcast(F32)
            xt = ps_x.tile([P, 2, 2, P], F32, name="xt")
            for b in range(2):
                for k in range(2):
                    nc.tensor.transpose(xt[:, b, k, :], words[:, 2 * h + b, k:256:2], ident[:])
            copy(
                eng,
                xgw[:, 256 * h : 256 * h + 256, :].rearrange("p (b n) k -> p b n k", b=2),
                xt[:].rearrange("p b k n -> p b n k"),
            )

        def xq_(u, r):
            c_ = st4.tile([P, 512], U32, name="xc", align_bytes=64)
            s_ = st4.tile([P, 512], U8, name="xs", align_bytes=64)
            quant(c_, s_[:], xgt[u, r])
            xq[u, r] = (c_, s_)

        def mm(out, lhs, lcols, rhs, first, last):
            nc.tensor.matmul_mx(
                out=out,
                lhsT=lhs[0][:, lcols].bitcast(FP8X4),
                lhsT_scale=lhs[1][:, lcols],
                rhs=rhs[0][:].bitcast(FP8X4),
                rhs_scale=rhs[1][:],
                start=first,
                stop=last,
            )

        def l1(u, r, t, eng):
            g = UNITS[u][0]
            if (u, r) not in hrt:
                hraw = st3.tile([P, 4, 512], BF16, name="hraw")
                hrt[u, r] = hraw
            wa, wb = ((1, 0, g), (1, 2, g)) if r == 0 else ((1, 1, g), (1, 0, g))
            cols = slice(P * t, P * t + P)
            acc = ps_1.tile([P, 512], F32, name="acc1")
            mm(acc[:], wq[wa], cols, xq[u, 0], True, False)
            mm(acc[:], wq[wb], cols, xq[u, 1], False, True)
            i = (r * G + g) * 4 + t
            if eng == "V":
                nc.vector.tensor_scalar(
                    out=hrt[u, r][:, t, :], in0=acc[:], scalar1=b1f[:, i : i + 1], scalar2=0.0, op0=ALU.add, op1=ALU.max
                )
            else:
                nc.scalar.activation(out=hrt[u, r][:, t, :], in_=acc[:], func=ACT.Relu, bias=b1f[:, i : i + 1])

        def hint(u, r, eng):
            hg = hgt[u, r] = st.tile([P, 512, 4], BF16, name="hg", align_bytes=64)
            interleave4(eng, hg[:], hrt[u, r][:])

        def hq_(u, r):
            c_ = st4.tile([P, 512], U32, name="hc", align_bytes=64)
            s_ = st4.tile([P, 512], U8, name="hs", align_bytes=64)
            quant(c_, s_[:], hgt[u, r])
            hq[u, r] = (c_, s_)

        def z_(u, r, t):
            g = UNITS[u][0]
            if (u, r) not in zt:
                z = st3.tile([P, 4, 512], F32, name="z")
                y = st4.tile([P, 4, 512], F32, name="y")
                zt[u, r] = z
                yt[u, r] = y
            wa, wb = ((2, 0, g), (2, 2, g)) if r == 0 else ((2, 1, g), (2, 0, g))
            m0 = (r * G + g) * 512
            cols = slice(P * t, P * t + P)
            acc = ps_2.tile([P, 512], F32, name="acc2")
            mm(acc[:], hq[u, 0], cols, wq[wa], True, False)
            mm(acc[:], hq[u, 1], cols, wq[wb], False, True)
            nc.vector.tensor_tensor(out=zt[u, r][:, t, :], in0=acc[:], in1=b2b[:, r, g, :], op=ALU.add)

        def p_(u, r, k, eng):
            h = slice(2 * k, 2 * k + 2)
            if eng in "VG":
                e = nc.vector if eng == "V" else nc.gpsimd
                e.tensor_scalar(
                    out=yt[u, r][:, h, :], in0=zt[u, r][:, h, :], scalar1=-THR, scalar2=0.0, op0=ALU.add, op1=ALU.max
                )
            else:
                nc.scalar.activation(out=yt[u, r][:, h, :], in_=zt[u, r][:, h, :], func=ACT.Relu, bias=-THR)

        def y_(u, r, k):
            h = slice(2 * k, 2 * k + 2)
            y = yt[u, r]
            nc.vector.scalar_tensor_tensor(
                out=y[:, h, :], in0=zt[u, r][:, h, :], scalar=THR, in1=y[:, h, :], op0=ALU.add, op1=ALU.min
            )

        def sty(u, r):
            g, a = UNITS[u]
            nc.sync.dma_start(
                out=out_0[r, g, 512 * a : 512 * a + 512, :].rearrange("(p t) d -> p t d", t=4), in_=yt[u, r][:]
            )

        def yint(u, r, k, eng):
            if (u, r) not in ygt:
                yg = st.tile([P, 512, 4], BF16, name="yg", align_bytes=64)
                ygt[u, r] = yg
            h = slice(256 * k, 256 * k + 256)
            if eng == "G":
                copy(eng, ygt[u, r][:, h, :], yt[u, r][:, :, h].rearrange("p t d -> p d t"))
            else:
                interleave4(eng, ygt[u, r][:, h, :], yt[u, r][:, :, h])

        def yq(u, r):
            g, a = UNITS[u]
            m0 = (r * G + g) * 512
            if u not in sct:
                ysc = st4.tile([P, 2, 512], U8, name="ysc", align_bytes=64)
                sct[u] = [ysc, 0]
            yc = st4.tile([P, 512], U32, name="yc", align_bytes=64)
            quant(yc, sct[u][0][:, r, :], ygt[u, r])
            nc.sync.dma_start(
                out=out_1[a, :, m0 : m0 + 512, :].rearrange("p m j -> p (m j)").bitcast(I32), in_=yc[:].bitcast(I32)
            )
            sct[u][1] += 1
            if sct[u][1] == 2:
                o2 = out_2[a, :, :].rearrange("q (r g d) -> q r g d", r=R, g=G)
                for q in range(4):
                    eng = nc.scalar if u == 3 and q % 2 else nc.sync
                    eng.dma_start(
                        out=o2[4 * q : 4 * q + 4, :, g, :].bitcast(I32),
                        in_=sct[u][0][32 * q : 32 * q + 4, :, :].bitcast(I32),
                    )

        steps = {"wint": wint, "wq": wq_, "neg": neg, "nq": nq, "x": x_, "xq": xq_, "l1": l1, "hint": hint, "hq": hq_,
                 "z": z_, "p": p_, "y": y_, "sty": sty, "yint": yint, "yq": yq}
        for word in ORDER.split():
            parts = word.split(":")
            args = [s if s in ("V", "S", "G") else int(s) for s in parts[1].split(",")]
            steps[parts[0]](*args)
